import numpy as np
import ml_dtypes


def mxq(x, axis, fmt="e4m3"):
    dtype, down = {"e4m3": (ml_dtypes.float8_e4m3fn, 7), "e5m2": (ml_dtypes.float8_e5m2, 14)}[fmt]
    v = np.moveaxis(np.asarray(x, np.float32).astype(ml_dtypes.bfloat16).astype(np.float64), axis, -1)
    blocks = v.reshape(v.shape[:-1] + (-1, 32))
    amax = np.abs(blocks).max(-1, keepdims=True)
    byte = np.maximum(np.where(amax > 0, np.frexp(amax)[1] - 1 + 127, 0) - down, 1)
    scale = np.exp2(byte - 127.0)
    codes = (blocks / scale).astype(np.float32).astype(dtype).astype(np.float64)
    return np.moveaxis((codes * scale).reshape(v.shape), -1, axis)


WIDE = False


def mx_kscale(k, group=512):
    if not WIDE:
        return np.ones(k)
    levels = np.array([10, -10, 5, -5, 0])
    if group != 512:
        return np.exp2(np.random.permutation(np.resize(levels, k // group))).repeat(group)
    if k % 512:
        return np.exp2(np.random.permutation(np.resize(levels, k // 32))).repeat(32)
    a = np.empty((k // 512, 16))
    for p in range(k // 512):
        a[p, :8] = np.random.permutation(np.resize(levels, 8))
        for g in range(8):
            far = levels[np.abs(levels - a[p, g]) >= 10]
            a[p, g + 8] = far[np.random.randint(len(far))]
    return np.exp2(a.ravel()).repeat(32)


def f64(x):
    return np.asarray(x).astype(np.float64)


def gelu(v):
    return 0.5 * v * (1.0 + np.tanh(0.7978845608028654 * (v + 0.044715 * v ** 3)))


def bf(x):
    return np.asarray(x, np.float32).astype(ml_dtypes.bfloat16)


def planes(Y):
    r, m = Y.shape
    b = f64(bf(Y)).reshape(r // 32, 32, m)
    amax = np.abs(b).max(1)
    byte = np.clip(np.where(amax > 0, np.frexp(amax)[1] - 1 + 127 - 7, 1), 1, 254)
    codes = (b * np.exp2(127.0 - byte)[:, None, :]).reshape(r, m).astype(np.float32).astype(ml_dtypes.float8_e4m3fn).view(np.uint8)
    words = codes.reshape(r // 512, 128, 4, m).transpose(0, 1, 3, 2)
    return np.ascontiguousarray(words), np.ascontiguousarray(byte.astype(np.uint8).reshape(r // 512, 16, m))


G, D, M, N = 2, 256, 256, 512


def setup_inputs():
    n = np.random.standard_normal
    s_d = mx_kscale(D, 0)
    return {
        "x": (n((G, D, N)) * s_d[:, None]).astype(np.float32),
        "w": (n((G, D, M)) / np.sqrt(D) / s_d[:, None]).astype(np.float32),
        "r": (n((G, M, N))).astype(np.float32),
    }


def reference(x, w, r):
    wq = mxq(f64(w), 1, "e4m3")
    xq = mxq(f64(x), 1, "e4m3")
    z = wq.transpose(0, 2, 1) @ xq
    y = gelu(z) + f64(r)
    Y = y.reshape(G * M, N)
    words, scales = planes(Y)
    return Y, words, scales

@@ -1,0 +1,141 @@
+from contextlib import ExitStack
+
+import concourse.mybir as mybir
+
+G, D, M, N = 2, 256, 256, 512
+FLOPS = 2 * G * D * M * N
+
+F32 = mybir.dt.float32
+BF16 = mybir.dt.bfloat16
+U32 = mybir.dt.uint32
+I32 = mybir.dt.int32
+U8 = mybir.dt.uint8
+FP8X4 = mybir.dt.float8_e4m3fn_x4
+GELU = mybir.ActivationFunctionType.Gelu_apprx_tanh
+ADD = mybir.AluOpType.add
+
+P = 128
+R = 64
+PACK = 4
+CH = 128
+NCH = N // CH
+HALF = N // 2
+
+
+def tile_rows_pl_ggelu_kernel(tc, x, w, r, out_0, out_1, out_2):
+    nc = tc.nc
+    x_rows = x.rearrange("g (p j) n -> (g p) j n", j=PACK)
+    w_rows = w.rearrange("g (p j) m -> (g p) j m", j=PACK)
+    r_rows = r.rearrange("g (p t) n -> (g p) t n", t=PACK)
+    y_rows = out_0.rearrange("(p t) n -> p t n", t=PACK)
+    word_rows = out_1.rearrange("s p n u -> p (s n u)").bitcast(I32)
+    scale_rows = out_2.rearrange("s f n -> (s f) n").bitcast(I32)
+
+    with ExitStack() as ctx:
+        sb = ctx.enter_context(tc.tile_pool(name="sb", bufs=1))
+        ps = ctx.enter_context(tc.psum_pool(name="ps", bufs=1))
+        ctx.enter_context(tc.manual_schedule())
+
+        w_raw = sb.tile([P, PACK, M], F32, name="w_raw")
+        nc.sync.dma_start(out=w_raw[:], in_=w_rows)
+        x_raw = []
+        r_raw = []
+        for h in range(2):
+            xt = sb.tile([P, PACK, HALF], F32, name="x_raw%d" % h)
+            nc.sync.dma_start(out=xt[:], in_=x_rows[:, :, h * HALF:(h + 1) * HALF])
+            x_raw.append(xt)
+        for h in range(2):
+            rt = sb.tile([P, PACK, HALF], F32, name="r_raw%d" % h)
+            nc.sync.dma_start(out=rt[:], in_=r_rows[:, :, h * HALF:(h + 1) * HALF])
+            r_raw.append(rt)
+
+        w_codes = sb.tile([P, M + 2 * R], U32, name="w_codes", align_bytes=64)
+        w_scales = sb.tile([P, M + 2 * R], U8, name="w_scales", align_bytes=64)
+        nc.vector.memset(w_codes[:], 0)
+        nc.vector.memset(w_scales[:].bitcast(U32), 0)
+        w_bf = sb.tile([P, PACK, R, PACK], BF16, name="w_bf", align_bytes=64)
+        nc.vector.tensor_copy(
+            out=w_bf[:].rearrange("p t m j -> p m t j"),
+            in_=w_raw[:].rearrange("p j (m t) -> p m t j", t=PACK),
+        )
+        nc.vector.quantize_mx(
+            out=w_codes[:, R:R + M].bitcast(FP8X4),
+            scales=w_scales[:, R:R + M],
+            in_=w_bf[:].rearrange("p t m j -> p (t m j)"),
+        )
+
+        def interleave(dst, src):
+            nc.vector.tensor_copy(
+                out=dst.rearrange("p (c i) j -> p c j i", i=PACK),
+                in_=src.rearrange("p j (c i) -> p c j i", i=PACK),
+            )
+
+        def quantise(codes, scales, grouped):
+            nc.vector.quantize_mx(
+                out=codes.bitcast(FP8X4), scales=scales, in_=grouped.rearrange("p n j -> p (n j)")
+            )
+
+        x_bf = [sb.tile([P, CH, PACK], BF16, name="x_bf%d" % c, align_bytes=64) for c in range(NCH)]
+        x_codes = [sb.tile([P, CH], U32, name="x_codes%d" % c, align_bytes=64) for c in range(NCH)]
+        x_scales = [sb.tile([P, CH], U8, name="x_scales%d" % c, align_bytes=64) for c in range(NCH)]
+        for h in range(2):
+            for q in range(2):
+                interleave(x_bf[2 * h + q][:], x_raw[h][:, :, q * CH:(q + 1) * CH])
+            for q in range(2):
+                c = 2 * h + q
+                quantise(x_codes[c][:], x_scales[c][:], x_bf[c][:])
+
+        z = {}
+        for c in range(NCH):
+            for g in range(G):
+                bank = ps.tile([P, PACK, CH], F32, name="z%d_%d" % (c, g))
+                rows = slice(g * R, (g + 1) * R)
+                for t in range(PACK):
+                    first = R * (t + 1 - g)
+                    nc.tensor.matmul_mx(
+                        out=bank[:, t, :],
+                        lhsT=w_codes[rows, first:first + P].bitcast(FP8X4),
+                        lhsT_scale=w_scales[rows, first:first + P],
+                        rhs=x_codes[c][rows, :].bitcast(FP8X4),
+                        rhs_scale=x_scales[c][rows, :],
+                        start=True,
+                        stop=True,
+                    )
+                z[(c, g)] = bank
+
+        pieces = [(0, CH), (CH, CH), (2 * CH, CH), (3 * CH, CH // 2), (3 * CH + CH // 2, CH // 2)]
+        stores = {1: (0, 2 * CH), 2: (2 * CH, CH), 4: (3 * CH, CH)}
+        y = sb.tile([P, PACK, N], F32, name="y")
+        y_codes = sb.tile([P, N], U32, name="y_codes", align_bytes=64)
+        y_scales = sb.tile([P, N], U8, name="y_scales", align_bytes=64)
+        act = []
+        for i, (lo, width) in enumerate(pieces):
+            a = sb.tile([P, PACK, width], F32, name="act%d" % i)
+            c, off = divmod(lo, CH)
+            for g in range(G):
+                rows = slice(g * R, (g + 1) * R)
+                nc.scalar.activation(out=a[rows, :, :], in_=z[(c, g)][rows, :, off:off + width], func=GELU)
+            act.append(a)
+
+        y_bf = [sb.tile([P, width, PACK], BF16, name="y_bf%d" % i, align_bytes=64) for i, (lo, width) in enumerate(pieces)]
+
+        def quantise_y(i):
+            lo, width = pieces[i]
+            quantise(y_codes[:, lo:lo + width], y_scales[:, lo:lo + width], y_bf[i][:])
+
+        for i, (lo, width) in enumerate(pieces):
+            h, off = divmod(lo, HALF)
+            nc.vector.tensor_tensor(out=y[:, :, lo:lo + width], in0=act[i][:], in1=r_raw[h][:, :, off:off + width], op=ADD)
+            if i > 0:
+                quantise_y(i - 1)
+            interleave(y_bf[i][:], y[:, :, lo:lo + width])
+            if i == 3:
+                nc.sync.dma_start(out=word_rows[:, 0:3 * CH], in_=y_codes[:, 0:3 * CH].bitcast(I32))
+            if i in stores:
+                s0, sw = stores[i]
+                nc.sync.dma_start(out=y_rows[:, :, s0:s0 + sw], in_=y[:, :, s0:s0 + sw])
+        quantise_y(len(pieces) - 1)
+        nc.sync.dma_start(out=word_rows[:, 3 * CH:N], in_=y_codes[:, 3 * CH:N].bitcast(I32))
+        for q in range(4):
+            eng = nc.sync if q < 2 else nc.scalar
+            eng.dma_start(out=scale_rows[4 * q:4 * q + 4, :], in_=y_scales[32 * q:32 * q + 4, :].bitcast(I32))

@@ -36,16 +36,17 @@ def tile_rows_pl_ggelu_kernel(tc, x, w, r, out_0, out_1, out_2):
         ps = ctx.enter_context(tc.psum_pool(name="ps", bufs=1))
         ctx.enter_context(tc.manual_schedule())
 
-        w_raw = sb.tile([P, PACK, M], F32, name="w_raw")
+        w_raw = sb.tile([P, PACK, M], F32, name="w_raw", tag="raw_a")
         nc.sync.dma_start(out=w_raw[:], in_=w_rows)
         x_raw = []
         r_raw = []
         for h in range(2):
-            xt = sb.tile([P, PACK, HALF], F32, name="x_raw%d" % h)
+            xt = sb.tile([P, PACK, HALF], F32, name="x_raw%d" % h, tag="raw_x%d" % h)
             nc.sync.dma_start(out=xt[:], in_=x_rows[:, :, h * HALF:(h + 1) * HALF])
             x_raw.append(xt)
-        for h in range(2):
-            rt = sb.tile([P, PACK, HALF], F32, name="r_raw%d" % h)
+
+        def load_residual(h, tag):
+            rt = sb.tile([P, PACK, HALF], F32, name="r_raw%d" % h, tag=tag)
             nc.sync.dma_start(out=rt[:], in_=r_rows[:, :, h * HALF:(h + 1) * HALF])
             r_raw.append(rt)
 
@@ -58,6 +59,7 @@ def tile_rows_pl_ggelu_kernel(tc, x, w, r, out_0, out_1, out_2):
             out=w_bf[:].rearrange("p t m j -> p m t j"),
             in_=w_raw[:].rearrange("p j (m t) -> p m t j", t=PACK),
         )
+        load_residual(0, "raw_a")
         nc.vector.quantize_mx(
             out=w_codes[:, R:R + M].bitcast(FP8X4),
             scales=w_scales[:, R:R + M],
@@ -81,6 +83,8 @@ def tile_rows_pl_ggelu_kernel(tc, x, w, r, out_0, out_1, out_2):
         for h in range(2):
             for q in range(2):
                 interleave(x_bf[2 * h + q][:], x_raw[h][:, :, q * CH:(q + 1) * CH])
+            if h == 0:
+                load_residual(1, "raw_x0")
             for q in range(2):
                 c = 2 * h + q
                 quantise(x_codes[c][:], x_scales[c][:], x_bf[c][:])

@@ -92,12 +92,13 @@ def tile_rows_pl_ggelu_kernel(tc, x, w, r, out_0, out_1, out_2):
         z = {}
         for c in range(NCH):
             for g in range(G):
-                bank = ps.tile([P, PACK, CH], F32, name="z%d_%d" % (c, g))
-                rows = slice(g * R, (g + 1) * R)
-                for t in range(PACK):
+                z[(c, g)] = ps.tile([P, PACK, CH], F32, name="z%d_%d" % (c, g))
+            for t in range(PACK):
+                for g in range(G):
+                    rows = slice(g * R, (g + 1) * R)
                     first = R * (t + 1 - g)
                     nc.tensor.matmul_mx(
-                        out=bank[:, t, :],
+                        out=z[(c, g)][:, t, :],
                         lhsT=w_codes[rows, first:first + P].bitcast(FP8X4),
                         lhsT_scale=w_scales[rows, first:first + P],
                         rhs=x_codes[c][rows, :].bitcast(FP8X4),
@@ -105,7 +106,6 @@ def tile_rows_pl_ggelu_kernel(tc, x, w, r, out_0, out_1, out_2):
                         start=True,
                         stop=True,
                     )
-                z[(c, g)] = bank
 
         pieces = [(0, CH), (CH, CH), (2 * CH, CH), (3 * CH, CH // 2), (3 * CH + CH // 2, CH // 2)]
         stores = {1: (0, 2 * CH), 2: (2 * CH, CH), 4: (3 * CH, CH)}

@@ -20,6 +20,7 @@ PACK = 4
 CH = 128
 NCH = N // CH
 HALF = N // 2
+PAD = 16
 
 
 def tile_rows_pl_ggelu_kernel(tc, x, w, r, out_0, out_1, out_2):
@@ -41,8 +42,8 @@ def tile_rows_pl_ggelu_kernel(tc, x, w, r, out_0, out_1, out_2):
         x_raw = []
         r_raw = []
         for h in range(2):
-            xt = sb.tile([P, PACK, HALF], F32, name="x_raw%d" % h, tag="raw_x%d" % h)
-            nc.sync.dma_start(out=xt[:], in_=x_rows[:, :, h * HALF:(h + 1) * HALF])
+            xt = sb.tile([P, PACK, HALF + PAD], F32, name="x_raw%d" % h, tag="raw_x%d" % h)
+            nc.sync.dma_start(out=xt[:, :, 0:HALF], in_=x_rows[:, :, h * HALF:(h + 1) * HALF])
             x_raw.append(xt)
 
         def load_residual(h, tag):
@@ -109,7 +110,7 @@ def tile_rows_pl_ggelu_kernel(tc, x, w, r, out_0, out_1, out_2):
 
         pieces = [(0, CH), (CH, CH), (2 * CH, CH), (3 * CH, CH // 2), (3 * CH + CH // 2, CH // 2)]
         stores = {1: (0, 2 * CH), 2: (2 * CH, CH), 4: (3 * CH, CH)}
-        y = sb.tile([P, PACK, N], F32, name="y")
+        y = sb.tile([P, PACK, N + PAD], F32, name="y")
         y_codes = sb.tile([P, N], U32, name="y_codes", align_bytes=64)
         y_scales = sb.tile([P, N], U8, name="y_scales", align_bytes=64)
         act = []

@@ -90,12 +90,15 @@ def tile_rows_pl_ggelu_kernel(tc, x, w, r, out_0, out_1, out_2):
                 c = 2 * h + q
                 quantise(x_codes[c][:], x_scales[c][:], x_bf[c][:])
 
+        def group_order(step):
+            return (0, 1) if step % 2 == 0 else (1, 0)
+
         z = {}
         for c in range(NCH):
             for g in range(G):
                 z[(c, g)] = ps.tile([P, PACK, CH], F32, name="z%d_%d" % (c, g))
             for t in range(PACK):
-                for g in range(G):
+                for g in group_order(c):
                     rows = slice(g * R, (g + 1) * R)
                     first = R * (t + 1 - g)
                     nc.tensor.matmul_mx(
@@ -117,7 +120,7 @@ def tile_rows_pl_ggelu_kernel(tc, x, w, r, out_0, out_1, out_2):
         for i, (lo, width) in enumerate(pieces):
             a = sb.tile([P, PACK, width], F32, name="act%d" % i)
             c, off = divmod(lo, CH)
-            for g in range(G):
+            for g in group_order(i):
                 rows = slice(g * R, (g + 1) * R)
                 nc.scalar.activation(out=a[rows, :, :], in_=z[(c, g)][rows, :, off:off + width], func=GELU)
             act.append(a)

@@ -20,7 +20,6 @@ PACK = 4
 CH = 128
 NCH = N // CH
 HALF = N // 2
-PAD = 16
 
 
 def tile_rows_pl_ggelu_kernel(tc, x, w, r, out_0, out_1, out_2):
@@ -40,15 +39,15 @@ def tile_rows_pl_ggelu_kernel(tc, x, w, r, out_0, out_1, out_2):
         w_raw = sb.tile([P, PACK, M], F32, name="w_raw", tag="raw_a")
         nc.sync.dma_start(out=w_raw[:], in_=w_rows)
         x_raw = []
-        r_raw = []
         for h in range(2):
-            xt = sb.tile([P, PACK, HALF + PAD], F32, name="x_raw%d" % h, tag="raw_x%d" % h)
-            nc.sync.dma_start(out=xt[:, :, 0:HALF], in_=x_rows[:, :, h * HALF:(h + 1) * HALF])
+            xt = sb.tile([P, PACK, HALF], F32, name="x_raw%d" % h, tag="raw_x%d" % h)
+            nc.sync.dma_start(out=xt[:], in_=x_rows[:, :, h * HALF:(h + 1) * HALF])
             x_raw.append(xt)
+        r_raw = []
 
-        def load_residual(h, tag):
-            rt = sb.tile([P, PACK, HALF], F32, name="r_raw%d" % h, tag=tag)
-            nc.sync.dma_start(out=rt[:], in_=r_rows[:, :, h * HALF:(h + 1) * HALF])
+        def load_residual(pair, tag):
+            rt = sb.tile([P, 2, N], F32, name="r_raw%d" % pair, tag=tag)
+            nc.sync.dma_start(out=rt[:], in_=r_rows[:, 2 * pair:2 * pair + 2, :])
             r_raw.append(rt)
 
         w_codes = sb.tile([P, M + 2 * R], U32, name="w_codes", align_bytes=64)
@@ -67,12 +66,6 @@ def tile_rows_pl_ggelu_kernel(tc, x, w, r, out_0, out_1, out_2):
             in_=w_bf[:].rearrange("p t m j -> p (t m j)"),
         )
 
-        def interleave(dst, src):
-            nc.vector.tensor_copy(
-                out=dst.rearrange("p (c i) j -> p c j i", i=PACK),
-                in_=src.rearrange("p j (c i) -> p c j i", i=PACK),
-            )
-
         def quantise(codes, scales, grouped):
             nc.vector.quantize_mx(
                 out=codes.bitcast(FP8X4), scales=scales, in_=grouped.rearrange("p n j -> p (n j)")
@@ -83,26 +76,30 @@ def tile_rows_pl_ggelu_kernel(tc, x, w, r, out_0, out_1, out_2):
         x_scales = [sb.tile([P, CH], U8, name="x_scales%d" % c, align_bytes=64) for c in range(NCH)]
         for h in range(2):
             for q in range(2):
-                interleave(x_bf[2 * h + q][:], x_raw[h][:, :, q * CH:(q + 1) * CH])
+                nc.vector.tensor_copy(
+                    out=x_bf[2 * h + q][:].rearrange("p (c i) j -> p c j i", i=PACK),
+                    in_=x_raw[h][:, :, q * CH:(q + 1) * CH].rearrange("p j (c i) -> p c j i", i=PACK),
+                )
             if h == 0:
                 load_residual(1, "raw_x0")
             for q in range(2):
                 c = 2 * h + q
                 quantise(x_codes[c][:], x_scales[c][:], x_bf[c][:])
 
-        def group_order(step):
-            return (0, 1) if step % 2 == 0 else (1, 0)
-
+        pieces = [(pair, 2 * h + q) for h in range(2) for pair in range(2) for q in range(2)]
+        banks = [(0,), (1,), (2, 3), (4, 5), (6, 7)]
         z = {}
-        for c in range(NCH):
-            for g in range(G):
-                z[(c, g)] = ps.tile([P, PACK, CH], F32, name="z%d_%d" % (c, g))
-            for t in range(PACK):
-                for g in group_order(c):
-                    rows = slice(g * R, (g + 1) * R)
-                    first = R * (t + 1 - g)
+
+        def passes(b, g):
+            bank = ps.tile([P, len(banks[b]), 2, CH], F32, name="z%d_%d" % (b, g), tag="bank%d_%d" % (b % 4, g))
+            rows = slice(g * R, (g + 1) * R)
+            for k, i in enumerate(banks[b]):
+                pair, c = pieces[i]
+                z[(i, g)] = bank[:, k, :, :]
+                for s in range(2):
+                    first = R * (2 * pair + s + 1 - g)
                     nc.tensor.matmul_mx(
-                        out=z[(c, g)][:, t, :],
+                        out=bank[:, k, s, :],
                         lhsT=w_codes[rows, first:first + P].bitcast(FP8X4),
                         lhsT_scale=w_scales[rows, first:first + P],
                         rhs=x_codes[c][rows, :].bitcast(FP8X4),
@@ -111,39 +108,80 @@ def tile_rows_pl_ggelu_kernel(tc, x, w, r, out_0, out_1, out_2):
                         stop=True,
                     )
 
-        pieces = [(0, CH), (CH, CH), (2 * CH, CH), (3 * CH, CH // 2), (3 * CH + CH // 2, CH // 2)]
-        stores = {1: (0, 2 * CH), 2: (2 * CH, CH), 4: (3 * CH, CH)}
-        y = sb.tile([P, PACK, N + PAD], F32, name="y")
+        act = [sb.tile([P, 2, CH], F32, name="act%d" % i) for i in range(len(pieces))]
+
+        def gelu(step):
+            for g in (1, 0):
+                rows = slice(0, (g + 1) * R)
+                for i in (2 * step, 2 * step + 1):
+                    nc.scalar.activation(out=act[i][rows], in_=z[(i, g)][rows], func=GELU)
+
+        for g in (1, 0):
+            passes(0, g)
+            passes(1, g)
+        for b in (2, 3):
+            for g in (1, 0):
+                passes(b, g)
+        gelu(0)
+        for g in (1, 0):
+            passes(4, g)
+        for step in range(1, 4):
+            gelu(step)
+
+        y = sb.tile([P, PACK, N], F32, name="y")
+        y_bf = [sb.tile([P, CH, PACK], BF16, name="y_bf%d" % c, align_bytes=64) for c in range(NCH)]
         y_codes = sb.tile([P, N], U32, name="y_codes", align_bytes=64)
         y_scales = sb.tile([P, N], U8, name="y_scales", align_bytes=64)
-        act = []
-        for i, (lo, width) in enumerate(pieces):
-            a = sb.tile([P, PACK, width], F32, name="act%d" % i)
-            c, off = divmod(lo, CH)
-            for g in group_order(i):
-                rows = slice(g * R, (g + 1) * R)
-                nc.scalar.activation(out=a[rows, :, :], in_=z[(c, g)][rows, :, off:off + width], func=GELU)
-            act.append(a)
 
-        y_bf = [sb.tile([P, width, PACK], BF16, name="y_bf%d" % i, align_bytes=64) for i, (lo, width) in enumerate(pieces)]
+        def add(i):
+            pair, c = pieces[i]
+            cols = slice(c * CH, (c + 1) * CH)
+            nc.vector.tensor_tensor(
+                out=y[:, 2 * pair:2 * pair + 2, cols], in0=act[i][:], in1=r_raw[pair][:, :, cols], op=ADD
+            )
 
-        def quantise_y(i):
-            lo, width = pieces[i]
-            quantise(y_codes[:, lo:lo + width], y_scales[:, lo:lo + width], y_bf[i][:])
+        def round_pair(i):
+            pair, c = pieces[i]
+            nc.vector.tensor_copy(
+                out=y_bf[c][:, :, 2 * pair:2 * pair + 2],
+                in_=y[:, 2 * pair:2 * pair + 2, c * CH:(c + 1) * CH].rearrange("p s n -> p n s"),
+            )
 
-        for i, (lo, width) in enumerate(pieces):
-            h, off = divmod(lo, HALF)
-            nc.vector.tensor_tensor(out=y[:, :, lo:lo + width], in0=act[i][:], in1=r_raw[h][:, :, off:off + width], op=ADD)
-            if i > 0:
-                quantise_y(i - 1)
-            interleave(y_bf[i][:], y[:, :, lo:lo + width])
-            if i == 3:
-                nc.sync.dma_start(out=word_rows[:, 0:3 * CH], in_=y_codes[:, 0:3 * CH].bitcast(I32))
-            if i in stores:
-                s0, sw = stores[i]
-                nc.sync.dma_start(out=y_rows[:, :, s0:s0 + sw], in_=y[:, :, s0:s0 + sw])
-        quantise_y(len(pieces) - 1)
-        nc.sync.dma_start(out=word_rows[:, 3 * CH:N], in_=y_codes[:, 3 * CH:N].bitcast(I32))
+        def quantise_y(c):
+            cols = slice(c * CH, (c + 1) * CH)
+            quantise(y_codes[:, cols], y_scales[:, cols], y_bf[c][:])
+
+        def store_y(first, last, lo, hi):
+            nc.sync.dma_start(out=y_rows[:, first:last, lo:hi], in_=y[:, first:last, lo:hi])
+
+        def store_words(lo, hi):
+            nc.sync.dma_start(out=word_rows[:, lo:hi], in_=y_codes[:, lo:hi].bitcast(I32))
+
+        add(0)
+        add(1)
+        round_pair(0)
+        round_pair(1)
+        add(2)
+        add(3)
+        store_y(0, PACK, 0, HALF)
+        round_pair(2)
+        round_pair(3)
+        quantise_y(0)
+        add(4)
+        add(5)
+        store_y(0, 2, HALF, N)
+        round_pair(4)
+        quantise_y(1)
+        store_words(0, HALF)
+        round_pair(5)
+        add(6)
+        add(7)
+        store_y(2, PACK, HALF, N)
+        round_pair(6)
+        round_pair(7)
+        quantise_y(2)
+        quantise_y(3)
+        store_words(HALF, N)
         for q in range(4):
             eng = nc.sync if q < 2 else nc.scalar
             eng.dma_start(out=scale_rows[4 * q:4 * q + 4, :], in_=y_scales[32 * q:32 * q + 4, :].bitcast(I32))

@@ -36,55 +36,67 @@ def tile_rows_pl_ggelu_kernel(tc, x, w, r, out_0, out_1, out_2):
         ps = ctx.enter_context(tc.psum_pool(name="ps", bufs=1))
         ctx.enter_context(tc.manual_schedule())
 
-        w_raw = sb.tile([P, PACK, M], F32, name="w_raw", tag="raw_a")
+        x_raw = [sb.tile([P, PACK, HALF], F32, name="x_raw%d" % h, tag="raw_x%d" % h, align_bytes=64) for h in range(2)]
+        w_raw = sb.tile([P, PACK, M], F32, name="w_raw", tag="raw_w")
+        nc.sync.dma_start(out=x_raw[0][:], in_=x_rows[:, :, 0:HALF])
         nc.sync.dma_start(out=w_raw[:], in_=w_rows)
-        x_raw = []
-        for h in range(2):
-            xt = sb.tile([P, PACK, HALF], F32, name="x_raw%d" % h, tag="raw_x%d" % h)
-            nc.sync.dma_start(out=xt[:], in_=x_rows[:, :, h * HALF:(h + 1) * HALF])
-            x_raw.append(xt)
+        nc.sync.dma_start(out=x_raw[1][:], in_=x_rows[:, :, HALF:N])
         r_raw = []
 
         def load_residual(pair, tag):
-            rt = sb.tile([P, 2, N], F32, name="r_raw%d" % pair, tag=tag)
+            rt = sb.tile([P, 2, N], F32, name="r_raw%d" % pair, tag=tag, align_bytes=64)
             nc.sync.dma_start(out=rt[:], in_=r_rows[:, 2 * pair:2 * pair + 2, :])
             r_raw.append(rt)
-
-        w_codes = sb.tile([P, M + 2 * R], U32, name="w_codes", align_bytes=64)
-        w_scales = sb.tile([P, M + 2 * R], U8, name="w_scales", align_bytes=64)
-        nc.vector.memset(w_codes[:], 0)
-        nc.vector.memset(w_scales[:].bitcast(U32), 0)
-        w_bf = sb.tile([P, PACK, R, PACK], BF16, name="w_bf", align_bytes=64)
-        nc.vector.tensor_copy(
-            out=w_bf[:].rearrange("p t m j -> p m t j"),
-            in_=w_raw[:].rearrange("p j (m t) -> p m t j", t=PACK),
-        )
-        load_residual(0, "raw_a")
-        nc.vector.quantize_mx(
-            out=w_codes[:, R:R + M].bitcast(FP8X4),
-            scales=w_scales[:, R:R + M],
-            in_=w_bf[:].rearrange("p t m j -> p (t m j)"),
-        )
 
         def quantise(codes, scales, grouped):
             nc.vector.quantize_mx(
                 out=codes.bitcast(FP8X4), scales=scales, in_=grouped.rearrange("p n j -> p (n j)")
             )
 
-        x_bf = [sb.tile([P, CH, PACK], BF16, name="x_bf%d" % c, align_bytes=64) for c in range(NCH)]
+        w_codes = [sb.tile([P, 4 * R], U32, name="w_codes%d" % pair, align_bytes=64) for pair in range(2)]
+        w_scales = [sb.tile([P, 4 * R], U8, name="w_scales%d" % pair, align_bytes=64) for pair in range(2)]
+        for pair in range(2):
+            nc.vector.memset(w_codes[pair][:], 0)
+            nc.vector.memset(w_scales[pair][:].bitcast(U32), 0)
+
+        x_bf = [sb.tile([P, CH, PACK], BF16, name="x_bf%d" % c, tag="x_bf%d" % c, align_bytes=64) for c in range(NCH)]
         x_codes = [sb.tile([P, CH], U32, name="x_codes%d" % c, align_bytes=64) for c in range(NCH)]
         x_scales = [sb.tile([P, CH], U8, name="x_scales%d" % c, align_bytes=64) for c in range(NCH)]
-        for h in range(2):
-            for q in range(2):
-                nc.vector.tensor_copy(
-                    out=x_bf[2 * h + q][:].rearrange("p (c i) j -> p c j i", i=PACK),
-                    in_=x_raw[h][:, :, q * CH:(q + 1) * CH].rearrange("p j (c i) -> p c j i", i=PACK),
-                )
-            if h == 0:
-                load_residual(1, "raw_x0")
-            for q in range(2):
-                c = 2 * h + q
-                quantise(x_codes[c][:], x_scales[c][:], x_bf[c][:])
+
+        def round_x(c):
+            h, q = divmod(c, 2)
+            nc.vector.tensor_copy(
+                out=x_bf[c][:].rearrange("p (c i) j -> p c j i", i=PACK),
+                in_=x_raw[h][:, :, q * CH:(q + 1) * CH].rearrange("p j (c i) -> p c j i", i=PACK),
+            )
+
+        def quantise_x(c):
+            quantise(x_codes[c][:], x_scales[c][:], x_bf[c][:])
+
+        w_bf = [sb.tile([P, 2 * R, PACK], BF16, name="w_bf%d" % pair, align_bytes=64) for pair in range(2)]
+
+        def round_w(pair):
+            nc.vector.tensor_copy(
+                out=w_bf[pair][:].rearrange("p (t m) j -> p m t j", t=2),
+                in_=w_raw[:].rearrange("p j (m t) -> p m t j", t=PACK)[:, :, 2 * pair:2 * pair + 2, :],
+            )
+
+        def quantise_w(pair):
+            quantise(w_codes[pair][:, R:3 * R], w_scales[pair][:, R:3 * R], w_bf[pair][:])
+
+        round_x(0)
+        round_x(1)
+        load_residual(0, "raw_x0")
+        quantise_x(0)
+        load_residual(1, "x_bf0")
+        quantise_x(1)
+        for pair in range(2):
+            round_w(pair)
+            quantise_w(pair)
+        round_x(2)
+        round_x(3)
+        quantise_x(2)
+        quantise_x(3)
 
         pieces = [(pair, 2 * h + q) for h in range(2) for pair in range(2) for q in range(2)]
         banks = [(0,), (1,), (2, 3), (4, 5), (6, 7)]
@@ -97,11 +109,11 @@ def tile_rows_pl_ggelu_kernel(tc, x, w, r, out_0, out_1, out_2):
                 pair, c = pieces[i]
                 z[(i, g)] = bank[:, k, :, :]
                 for s in range(2):
-                    first = R * (2 * pair + s + 1 - g)
+                    first = R * (s + 1 - g)
                     nc.tensor.matmul_mx(
                         out=bank[:, k, s, :],
-                        lhsT=w_codes[rows, first:first + P].bitcast(FP8X4),
-                        lhsT_scale=w_scales[rows, first:first + P],
+                        lhsT=w_codes[pair][rows, first:first + P].bitcast(FP8X4),
+                        lhsT_scale=w_scales[pair][rows, first:first + P],
                         rhs=x_codes[c][rows, :].bitcast(FP8X4),
                         rhs_scale=x_scales[c][rows, :],
                         start=True,

@@ -159,6 +159,13 @@ def tile_rows_pl_ggelu_kernel(tc, x, w, r, out_0, out_1, out_2):
                 in_=y[:, 2 * pair:2 * pair + 2, c * CH:(c + 1) * CH].rearrange("p s n -> p n s"),
             )
 
+        def round_pair_on_scalar(i):
+            pair, c = pieces[i]
+            nc.scalar.copy(
+                out=y_bf[c][:, :, 2 * pair:2 * pair + 2],
+                in_=y[:, 2 * pair:2 * pair + 2, c * CH:(c + 1) * CH].rearrange("p s n -> p n s"),
+            )
+
         def quantise_y(c):
             cols = slice(c * CH, (c + 1) * CH)
             quantise(y_codes[:, cols], y_scales[:, cols], y_bf[c][:])
@@ -185,7 +192,7 @@ def tile_rows_pl_ggelu_kernel(tc, x, w, r, out_0, out_1, out_2):
         round_pair(4)
         quantise_y(1)
         store_words(0, HALF)
-        round_pair(5)
+        round_pair_on_scalar(5)
         add(6)
         add(7)
         store_y(2, PACK, HALF, N)

@@ -36,44 +36,49 @@ def tile_rows_pl_ggelu_kernel(tc, x, w, r, out_0, out_1, out_2):
         ps = ctx.enter_context(tc.psum_pool(name="ps", bufs=1))
         ctx.enter_context(tc.manual_schedule())
 
-        x_raw = [sb.tile([P, PACK, HALF], F32, name="x_raw%d" % h, tag="raw_x%d" % h, align_bytes=64) for h in range(2)]
-        w_raw = sb.tile([P, PACK, M], F32, name="w_raw", tag="raw_w")
-        nc.sync.dma_start(out=x_raw[0][:], in_=x_rows[:, :, 0:HALF])
-        nc.sync.dma_start(out=w_raw[:], in_=w_rows)
-        nc.sync.dma_start(out=x_raw[1][:], in_=x_rows[:, :, HALF:N])
-        r_raw = []
+        x_raw = {}
+        r_raw = {}
+        w_raw = sb.tile([P, PACK, M], F32, name="w_raw", tag="raw_w", align_bytes=64)
 
-        def load_residual(pair, tag):
-            rt = sb.tile([P, 2, N], F32, name="r_raw%d" % pair, tag=tag, align_bytes=64)
-            nc.sync.dma_start(out=rt[:], in_=r_rows[:, 2 * pair:2 * pair + 2, :])
-            r_raw.append(rt)
+        def load_w():
+            nc.sync.dma_start(out=w_raw[:], in_=w_rows)
+
+        def load_x(lo, n):
+            xt = sb.tile([P, PACK, n * CH], F32, name="x_raw%d" % lo, tag="raw_x%d" % lo, align_bytes=64)
+            nc.sync.dma_start(out=xt[:], in_=x_rows[:, :, lo * CH:(lo + n) * CH])
+            for q in range(n):
+                x_raw[lo + q] = xt[:, :, q * CH:(q + 1) * CH]
+
+        def load_residual(lo, n, tag):
+            rt = sb.tile([P, PACK, n * CH], F32, name="r_raw%d" % lo, tag=tag, align_bytes=64)
+            nc.sync.dma_start(out=rt[:], in_=r_rows[:, :, lo * CH:(lo + n) * CH])
+            for q in range(n):
+                r_raw[lo + q] = rt[:, :, q * CH:(q + 1) * CH]
+
+        def interleave(dst, src):
+            nc.vector.tensor_copy(
+                out=dst.rearrange("p (c i) j -> p c j i", i=PACK),
+                in_=src.rearrange("p j (c i) -> p c j i", i=PACK),
+            )
 
         def quantise(codes, scales, grouped):
             nc.vector.quantize_mx(
                 out=codes.bitcast(FP8X4), scales=scales, in_=grouped.rearrange("p n j -> p (n j)")
             )
 
+        load_w()
+        load_x(0, 2)
+        load_x(2, 2)
+
         w_codes = [sb.tile([P, 4 * R], U32, name="w_codes%d" % pair, align_bytes=64) for pair in range(2)]
         w_scales = [sb.tile([P, 4 * R], U8, name="w_scales%d" % pair, align_bytes=64) for pair in range(2)]
         for pair in range(2):
             nc.vector.memset(w_codes[pair][:], 0)
             nc.vector.memset(w_scales[pair][:].bitcast(U32), 0)
-
-        x_bf = [sb.tile([P, CH, PACK], BF16, name="x_bf%d" % c, tag="x_bf%d" % c, align_bytes=64) for c in range(NCH)]
+        w_bf = [sb.tile([P, 2 * R, PACK], BF16, name="w_bf%d" % pair, tag="w_bf%d" % pair, align_bytes=64) for pair in range(2)]
+        x_bf = {c: sb.tile([P, CH, PACK], BF16, name="x_bf%d" % c, align_bytes=64) for c in range(1, NCH)}
         x_codes = [sb.tile([P, CH], U32, name="x_codes%d" % c, align_bytes=64) for c in range(NCH)]
         x_scales = [sb.tile([P, CH], U8, name="x_scales%d" % c, align_bytes=64) for c in range(NCH)]
-
-        def round_x(c):
-            h, q = divmod(c, 2)
-            nc.vector.tensor_copy(
-                out=x_bf[c][:].rearrange("p (c i) j -> p c j i", i=PACK),
-                in_=x_raw[h][:, :, q * CH:(q + 1) * CH].rearrange("p j (c i) -> p c j i", i=PACK),
-            )
-
-        def quantise_x(c):
-            quantise(x_codes[c][:], x_scales[c][:], x_bf[c][:])
-
-        w_bf = [sb.tile([P, 2 * R, PACK], BF16, name="w_bf%d" % pair, align_bytes=64) for pair in range(2)]
 
         def round_w(pair):
             nc.vector.tensor_copy(
@@ -84,21 +89,38 @@ def tile_rows_pl_ggelu_kernel(tc, x, w, r, out_0, out_1, out_2):
         def quantise_w(pair):
             quantise(w_codes[pair][:, R:3 * R], w_scales[pair][:, R:3 * R], w_bf[pair][:])
 
-        round_x(0)
+        def round_x(c):
+            interleave(x_bf[c][:], x_raw[c])
+
+        x_bf_first = [sb.tile([P, R, PACK], BF16, name="x_bf_first%d" % k, align_bytes=64) for k in range(2)]
+
+        def round_first(k):
+            interleave(x_bf_first[k][:], x_raw[0][:, :, k * R:(k + 1) * R])
+
+        def quantise_first(k):
+            quantise(x_codes[0][:, k * R:(k + 1) * R], x_scales[0][:, k * R:(k + 1) * R], x_bf_first[k][:])
+
+        def quantise_x(c):
+            quantise(x_codes[c][:], x_scales[c][:], x_bf[c][:])
+
+        round_w(0)
+        round_w(1)
+        load_residual(0, 2, "raw_w")
+        quantise_w(0)
+        quantise_w(1)
+        round_first(0)
+        round_first(1)
+        quantise_first(0)
+        quantise_first(1)
         round_x(1)
-        load_residual(0, "raw_x0")
-        quantise_x(0)
-        load_residual(1, "x_bf0")
+        load_residual(2, 2, "raw_x0")
         quantise_x(1)
-        for pair in range(2):
-            round_w(pair)
-            quantise_w(pair)
         round_x(2)
         round_x(3)
         quantise_x(2)
         quantise_x(3)
 
-        pieces = [(pair, 2 * h + q) for h in range(2) for pair in range(2) for q in range(2)]
+        pieces = [(0, 0), (1, 0), (0, 1), (1, 1), (0, 2), (0, 3), (1, 2), (1, 3)]
         banks = [(0,), (1,), (2, 3), (4, 5), (6, 7)]
         z = {}
 
@@ -147,10 +169,15 @@ def tile_rows_pl_ggelu_kernel(tc, x, w, r, out_0, out_1, out_2):
 
         def add(i):
             pair, c = pieces[i]
-            cols = slice(c * CH, (c + 1) * CH)
             nc.vector.tensor_tensor(
-                out=y[:, 2 * pair:2 * pair + 2, cols], in0=act[i][:], in1=r_raw[pair][:, :, cols], op=ADD
+                out=y[:, 2 * pair:2 * pair + 2, c * CH:(c + 1) * CH],
+                in0=act[i][:],
+                in1=r_raw[c][:, 2 * pair:2 * pair + 2, :],
+                op=ADD,
             )
+
+        def round_chunk(c):
+            interleave(y_bf[c][:], y[:, :, c * CH:(c + 1) * CH])
 
         def round_pair(i):
             pair, c = pieces[i]
@@ -178,14 +205,13 @@ def tile_rows_pl_ggelu_kernel(tc, x, w, r, out_0, out_1, out_2):
 
         add(0)
         add(1)
-        round_pair(0)
-        round_pair(1)
+        store_y(0, PACK, 0, CH)
+        round_chunk(0)
         add(2)
         add(3)
-        store_y(0, PACK, 0, HALF)
-        round_pair(2)
-        round_pair(3)
+        store_y(0, PACK, CH, HALF)
         quantise_y(0)
+        round_chunk(1)
         add(4)
         add(5)
         store_y(0, 2, HALF, N)

@@ -20,6 +20,7 @@ PACK = 4
 CH = 128
 NCH = N // CH
 HALF = N // 2
+PAD = 16
 
 
 def tile_rows_pl_ggelu_kernel(tc, x, w, r, out_0, out_1, out_2):
@@ -44,8 +45,8 @@ def tile_rows_pl_ggelu_kernel(tc, x, w, r, out_0, out_1, out_2):
             nc.sync.dma_start(out=w_raw[:], in_=w_rows)
 
         def load_x(lo, n):
-            xt = sb.tile([P, PACK, n * CH], F32, name="x_raw%d" % lo, tag="raw_x%d" % lo, align_bytes=64)
-            nc.sync.dma_start(out=xt[:], in_=x_rows[:, :, lo * CH:(lo + n) * CH])
+            xt = sb.tile([P, PACK, n * CH + PAD], F32, name="x_raw%d" % lo, tag="raw_x%d" % lo, align_bytes=64)
+            nc.sync.dma_start(out=xt[:, :, 0:n * CH], in_=x_rows[:, :, lo * CH:(lo + n) * CH])
             for q in range(n):
                 x_raw[lo + q] = xt[:, :, q * CH:(q + 1) * CH]
 
@@ -69,25 +70,25 @@ def tile_rows_pl_ggelu_kernel(tc, x, w, r, out_0, out_1, out_2):
         load_w()
         load_x(0, 2)
         load_x(2, 2)
+        load_residual(0, 2, "r0")
 
-        w_codes = [sb.tile([P, 4 * R], U32, name="w_codes%d" % pair, align_bytes=64) for pair in range(2)]
-        w_scales = [sb.tile([P, 4 * R], U8, name="w_scales%d" % pair, align_bytes=64) for pair in range(2)]
-        for pair in range(2):
-            nc.vector.memset(w_codes[pair][:], 0)
-            nc.vector.memset(w_scales[pair][:].bitcast(U32), 0)
-        w_bf = [sb.tile([P, 2 * R, PACK], BF16, name="w_bf%d" % pair, tag="w_bf%d" % pair, align_bytes=64) for pair in range(2)]
+        w_codes = sb.tile([P, M + 2 * R], U32, name="w_codes", align_bytes=64)
+        w_scales = sb.tile([P, M + 2 * R], U8, name="w_scales", align_bytes=64)
+        nc.vector.memset(w_codes[:], 0)
+        nc.vector.memset(w_scales[:].bitcast(U32), 0)
+        w_bf = sb.tile([P, PACK, R, PACK], BF16, name="w_bf", align_bytes=64)
         x_bf = {c: sb.tile([P, CH, PACK], BF16, name="x_bf%d" % c, align_bytes=64) for c in range(1, NCH)}
         x_codes = [sb.tile([P, CH], U32, name="x_codes%d" % c, align_bytes=64) for c in range(NCH)]
         x_scales = [sb.tile([P, CH], U8, name="x_scales%d" % c, align_bytes=64) for c in range(NCH)]
 
-        def round_w(pair):
+        def round_w():
             nc.vector.tensor_copy(
-                out=w_bf[pair][:].rearrange("p (t m) j -> p m t j", t=2),
-                in_=w_raw[:].rearrange("p j (m t) -> p m t j", t=PACK)[:, :, 2 * pair:2 * pair + 2, :],
+                out=w_bf[:].rearrange("p t m j -> p m t j"),
+                in_=w_raw[:].rearrange("p j (m t) -> p m t j", t=PACK),
             )
 
-        def quantise_w(pair):
-            quantise(w_codes[pair][:, R:3 * R], w_scales[pair][:, R:3 * R], w_bf[pair][:])
+        def quantise_w():
+            quantise(w_codes[:, R:R + M], w_scales[:, R:R + M], w_bf[:].rearrange("p t m j -> p (t m) j"))
 
         def round_x(c):
             interleave(x_bf[c][:], x_raw[c])
@@ -103,17 +104,14 @@ def tile_rows_pl_ggelu_kernel(tc, x, w, r, out_0, out_1, out_2):
         def quantise_x(c):
             quantise(x_codes[c][:], x_scales[c][:], x_bf[c][:])
 
-        round_w(0)
-        round_w(1)
-        load_residual(0, 2, "raw_w")
-        quantise_w(0)
-        quantise_w(1)
+        round_w()
+        load_residual(2, 2, "raw_w")
+        quantise_w()
         round_first(0)
         round_first(1)
         quantise_first(0)
         quantise_first(1)
         round_x(1)
-        load_residual(2, 2, "raw_x0")
         quantise_x(1)
         round_x(2)
         round_x(3)
@@ -131,11 +129,11 @@ def tile_rows_pl_ggelu_kernel(tc, x, w, r, out_0, out_1, out_2):
                 pair, c = pieces[i]
                 z[(i, g)] = bank[:, k, :, :]
                 for s in range(2):
-                    first = R * (s + 1 - g)
+                    first = R * (2 * pair + s + 1 - g)
                     nc.tensor.matmul_mx(
                         out=bank[:, k, s, :],
-                        lhsT=w_codes[pair][rows, first:first + P].bitcast(FP8X4),
-                        lhsT_scale=w_scales[pair][rows, first:first + P],
+                        lhsT=w_codes[rows, first:first + P].bitcast(FP8X4),
+                        lhsT_scale=w_scales[rows, first:first + P],
                         rhs=x_codes[c][rows, :].bitcast(FP8X4),
                         rhs_scale=x_scales[c][rows, :],
                         start=True,
@@ -162,7 +160,7 @@ def tile_rows_pl_ggelu_kernel(tc, x, w, r, out_0, out_1, out_2):
         for step in range(1, 4):
             gelu(step)
 
-        y = sb.tile([P, PACK, N], F32, name="y")
+        y = sb.tile([P, PACK, N + PAD], F32, name="y")
         y_bf = [sb.tile([P, CH, PACK], BF16, name="y_bf%d" % c, align_bytes=64) for c in range(NCH)]
         y_codes = sb.tile([P, N], U32, name="y_codes", align_bytes=64)
         y_scales = sb.tile([P, N], U8, name="y_scales", align_bytes=64)
@@ -186,13 +184,6 @@ def tile_rows_pl_ggelu_kernel(tc, x, w, r, out_0, out_1, out_2):
                 in_=y[:, 2 * pair:2 * pair + 2, c * CH:(c + 1) * CH].rearrange("p s n -> p n s"),
             )
 
-        def round_pair_on_scalar(i):
-            pair, c = pieces[i]
-            nc.scalar.copy(
-                out=y_bf[c][:, :, 2 * pair:2 * pair + 2],
-                in_=y[:, 2 * pair:2 * pair + 2, c * CH:(c + 1) * CH].rearrange("p s n -> p n s"),
-            )
-
         def quantise_y(c):
             cols = slice(c * CH, (c + 1) * CH)
             quantise(y_codes[:, cols], y_scales[:, cols], y_bf[c][:])
@@ -205,11 +196,10 @@ def tile_rows_pl_ggelu_kernel(tc, x, w, r, out_0, out_1, out_2):
 
         add(0)
         add(1)
-        store_y(0, PACK, 0, CH)
         round_chunk(0)
         add(2)
         add(3)
-        store_y(0, PACK, CH, HALF)
+        store_y(0, PACK, 0, HALF)
         quantise_y(0)
         round_chunk(1)
         add(4)
@@ -218,7 +208,7 @@ def tile_rows_pl_ggelu_kernel(tc, x, w, r, out_0, out_1, out_2):
         round_pair(4)
         quantise_y(1)
         store_words(0, HALF)
-        round_pair_on_scalar(5)
+        round_pair(5)
         add(6)
         add(7)
         store_y(2, PACK, HALF, N)

@@ -54,7 +54,14 @@ def tile_rows_pl_ggelu_kernel(tc, x, w, r, out_0, out_1, out_2):
             rt = sb.tile([P, PACK, n * CH], F32, name="r_raw%d" % lo, tag=tag, align_bytes=64)
             nc.sync.dma_start(out=rt[:], in_=r_rows[:, :, lo * CH:(lo + n) * CH])
             for q in range(n):
-                r_raw[lo + q] = rt[:, :, q * CH:(q + 1) * CH]
+                for pair in range(2):
+                    r_raw[(pair, lo + q)] = rt[:, 2 * pair:2 * pair + 2, q * CH:(q + 1) * CH]
+
+        def load_pair(pair, tag):
+            rt = sb.tile([P, 2, HALF], F32, name="r_first%d" % pair, tag=tag, align_bytes=64)
+            nc.sync.dma_start(out=rt[:], in_=r_rows[:, 2 * pair:2 * pair + 2, 0:HALF])
+            for c in range(2):
+                r_raw[(pair, c)] = rt[:, :, c * CH:(c + 1) * CH]
 
         def interleave(dst, src):
             nc.vector.tensor_copy(
@@ -70,7 +77,6 @@ def tile_rows_pl_ggelu_kernel(tc, x, w, r, out_0, out_1, out_2):
         load_w()
         load_x(0, 2)
         load_x(2, 2)
-        load_residual(0, 2, "r0")
 
         w_codes = sb.tile([P, M + 2 * R], U32, name="w_codes", align_bytes=64)
         w_scales = sb.tile([P, M + 2 * R], U8, name="w_scales", align_bytes=64)
@@ -105,13 +111,15 @@ def tile_rows_pl_ggelu_kernel(tc, x, w, r, out_0, out_1, out_2):
             quantise(x_codes[c][:], x_scales[c][:], x_bf[c][:])
 
         round_w()
-        load_residual(2, 2, "raw_w")
+        load_pair(0, "raw_w")
+        load_pair(1, "raw_r")
         quantise_w()
         round_first(0)
         round_first(1)
         quantise_first(0)
         quantise_first(1)
         round_x(1)
+        load_residual(2, 2, "raw_x0")
         quantise_x(1)
         round_x(2)
         round_x(3)
@@ -170,7 +178,7 @@ def tile_rows_pl_ggelu_kernel(tc, x, w, r, out_0, out_1, out_2):
             nc.vector.tensor_tensor(
                 out=y[:, 2 * pair:2 * pair + 2, c * CH:(c + 1) * CH],
                 in0=act[i][:],
-                in1=r_raw[c][:, 2 * pair:2 * pair + 2, :],
+                in1=r_raw[(pair, c)],
                 op=ADD,
             )
 

@@ -223,8 +223,9 @@ def tile_rows_pl_ggelu_kernel(tc, x, w, r, out_0, out_1, out_2):
         round_pair(6)
         round_pair(7)
         quantise_y(2)
+        store_words(HALF, N - CH)
         quantise_y(3)
-        store_words(HALF, N)
+        store_words(N - CH, N)
         for q in range(4):
             eng = nc.sync if q < 2 else nc.scalar
             eng.dma_start(out=scale_rows[4 * q:4 * q + 4, :], in_=y_scales[32 * q:32 * q + 4, :].bitcast(I32))

@@ -50,18 +50,18 @@ def tile_rows_pl_ggelu_kernel(tc, x, w, r, out_0, out_1, out_2):
             for q in range(n):
                 x_raw[lo + q] = xt[:, :, q * CH:(q + 1) * CH]
 
-        def load_residual(lo, n, tag):
-            rt = sb.tile([P, PACK, n * CH], F32, name="r_raw%d" % lo, tag=tag, align_bytes=64)
-            nc.sync.dma_start(out=rt[:], in_=r_rows[:, :, lo * CH:(lo + n) * CH])
-            for q in range(n):
-                for pair in range(2):
-                    r_raw[(pair, lo + q)] = rt[:, 2 * pair:2 * pair + 2, q * CH:(q + 1) * CH]
-
-        def load_pair(pair, tag):
-            rt = sb.tile([P, 2, HALF], F32, name="r_first%d" % pair, tag=tag, align_bytes=64)
-            nc.sync.dma_start(out=rt[:], in_=r_rows[:, 2 * pair:2 * pair + 2, 0:HALF])
+        def load_pair(pair, h, tag):
+            rt = sb.tile([P, 2, HALF], F32, name="r_raw%d_%d" % (pair, h), tag=tag, align_bytes=64)
+            nc.sync.dma_start(out=rt[:], in_=r_rows[:, 2 * pair:2 * pair + 2, h * HALF:(h + 1) * HALF])
             for c in range(2):
-                r_raw[(pair, c)] = rt[:, :, c * CH:(c + 1) * CH]
+                r_raw[(pair, 2 * h + c)] = rt[:, :, c * CH:(c + 1) * CH]
+
+        def load_second_half(tag):
+            rt = sb.tile([P, PACK, HALF], F32, name="r_second", tag=tag, align_bytes=64)
+            nc.sync.dma_start(out=rt[:], in_=r_rows[:, :, HALF:N])
+            for pair in range(2):
+                for c in range(2):
+                    r_raw[(pair, 2 + c)] = rt[:, 2 * pair:2 * pair + 2, c * CH:(c + 1) * CH]
 
         def interleave(dst, src):
             nc.vector.tensor_copy(
@@ -93,8 +93,10 @@ def tile_rows_pl_ggelu_kernel(tc, x, w, r, out_0, out_1, out_2):
                 in_=w_raw[:].rearrange("p j (m t) -> p m t j", t=PACK),
             )
 
-        def quantise_w():
-            quantise(w_codes[:, R:R + M], w_scales[:, R:R + M], w_bf[:].rearrange("p t m j -> p (t m) j"))
+        def quantise_w(pair):
+            cols = slice(R + pair * P, R + (pair + 1) * P)
+            slices = w_bf[:, 2 * pair:2 * pair + 2]
+            quantise(w_codes[:, cols], w_scales[:, cols], slices.rearrange("p t m j -> p (t m) j"))
 
         def round_x(c):
             interleave(x_bf[c][:], x_raw[c])
@@ -111,15 +113,16 @@ def tile_rows_pl_ggelu_kernel(tc, x, w, r, out_0, out_1, out_2):
             quantise(x_codes[c][:], x_scales[c][:], x_bf[c][:])
 
         round_w()
-        load_pair(0, "raw_w")
-        load_pair(1, "raw_r")
-        quantise_w()
+        load_pair(0, 0, "raw_w")
+        load_pair(1, 0, "raw_r0")
+        quantise_w(0)
         round_first(0)
         round_first(1)
+        quantise_w(1)
         quantise_first(0)
         quantise_first(1)
         round_x(1)
-        load_residual(2, 2, "raw_x0")
+        load_second_half("raw_x0")
         quantise_x(1)
         round_x(2)
         round_x(3)
@@ -127,19 +130,22 @@ def tile_rows_pl_ggelu_kernel(tc, x, w, r, out_0, out_1, out_2):
         quantise_x(3)
 
         pieces = [(0, 0), (1, 0), (0, 1), (1, 1), (0, 2), (0, 3), (1, 2), (1, 3)]
-        banks = [(0,), (1,), (2, 3), (4, 5), (6, 7)]
         z = {}
+        opened = [0, 0]
 
-        def passes(b, g):
-            bank = ps.tile([P, len(banks[b]), 2, CH], F32, name="z%d_%d" % (b, g), tag="bank%d_%d" % (b % 4, g))
+        def passes(g, todo, slots=(0, 1)):
+            bank = ps.tile(
+                [P, len(todo), len(slots), CH], F32, name="z%d_%d" % (opened[g], g), tag="bank%d_%d" % (opened[g] % 4, g)
+            )
+            opened[g] = opened[g] + 1
             rows = slice(g * R, (g + 1) * R)
-            for k, i in enumerate(banks[b]):
+            for k, i in enumerate(todo):
                 pair, c = pieces[i]
-                z[(i, g)] = bank[:, k, :, :]
-                for s in range(2):
+                z[(i, g, slots)] = bank[:, k, :, :]
+                for n, s in enumerate(slots):
                     first = R * (2 * pair + s + 1 - g)
                     nc.tensor.matmul_mx(
-                        out=bank[:, k, s, :],
+                        out=bank[:, k, n, :],
                         lhsT=w_codes[rows, first:first + P].bitcast(FP8X4),
                         lhsT_scale=w_scales[rows, first:first + P],
                         rhs=x_codes[c][rows, :].bitcast(FP8X4),
@@ -150,23 +156,22 @@ def tile_rows_pl_ggelu_kernel(tc, x, w, r, out_0, out_1, out_2):
 
         act = [sb.tile([P, 2, CH], F32, name="act%d" % i) for i in range(len(pieces))]
 
-        def gelu(step):
-            for g in (1, 0):
-                rows = slice(0, (g + 1) * R)
-                for i in (2 * step, 2 * step + 1):
-                    nc.scalar.activation(out=act[i][rows], in_=z[(i, g)][rows], func=GELU)
+        def gelu(i, g, slots=(0, 1)):
+            rows = slice(0, (g + 1) * R)
+            nc.scalar.activation(out=act[i][rows, slots[0]:slots[-1] + 1], in_=z[(i, g, slots)][rows], func=GELU)
 
-        for g in (1, 0):
-            passes(0, g)
-            passes(1, g)
-        for b in (2, 3):
-            for g in (1, 0):
-                passes(b, g)
-        gelu(0)
-        for g in (1, 0):
-            passes(4, g)
+        for s in range(2):
+            passes(1, (0,), (s,))
+            gelu(0, 1, (s,))
+        for g, i in ((1, 1), (0, 0), (0, 1)):
+            passes(g, (i,))
+            gelu(i, g)
         for step in range(1, 4):
-            gelu(step)
+            todo = (2 * step, 2 * step + 1)
+            for g in (1, 0):
+                passes(g, todo)
+                for i in todo:
+                    gelu(i, g)
 
         y = sb.tile([P, PACK, N + PAD], F32, name="y")
         y_bf = [sb.tile([P, CH, PACK], BF16, name="y_bf%d" % c, align_bytes=64) for c in range(NCH)]
@@ -206,8 +211,9 @@ def tile_rows_pl_ggelu_kernel(tc, x, w, r, out_0, out_1, out_2):
         add(1)
         round_chunk(0)
         add(2)
+        store_y(0, 2, 0, HALF)
         add(3)
-        store_y(0, PACK, 0, HALF)
+        store_y(2, PACK, 0, HALF)
         quantise_y(0)
         round_chunk(1)
         add(4)
@@ -223,9 +229,8 @@ def tile_rows_pl_ggelu_kernel(tc, x, w, r, out_0, out_1, out_2):
         round_pair(6)
         round_pair(7)
         quantise_y(2)
-        store_words(HALF, N - CH)
         quantise_y(3)
-        store_words(N - CH, N)
+        store_words(HALF, N)
         for q in range(4):
             eng = nc.sync if q < 2 else nc.scalar
             eng.dma_start(out=scale_rows[4 * q:4 * q + 4, :], in_=y_scales[32 * q:32 * q + 4, :].bitcast(I32))

@@ -168,8 +168,10 @@ def tile_rows_pl_ggelu_kernel(tc, x, w, r, out_0, out_1, out_2):
             gelu(i, g)
         for step in range(1, 4):
             todo = (2 * step, 2 * step + 1)
+            for i in todo:
+                for g in (0, 1):
+                    passes(g, (i,))
             for g in (1, 0):
-                passes(g, todo)
                 for i in todo:
                     gelu(i, g)
 
@@ -211,9 +213,8 @@ def tile_rows_pl_ggelu_kernel(tc, x, w, r, out_0, out_1, out_2):
         add(1)
         round_chunk(0)
         add(2)
-        store_y(0, 2, 0, HALF)
         add(3)
-        store_y(2, PACK, 0, HALF)
+        store_y(0, PACK, 0, HALF)
         quantise_y(0)
         round_chunk(1)
         add(4)
@@ -229,8 +230,9 @@ def tile_rows_pl_ggelu_kernel(tc, x, w, r, out_0, out_1, out_2):
         round_pair(6)
         round_pair(7)
         quantise_y(2)
+        store_words(HALF, N - CH)
         quantise_y(3)
-        store_words(HALF, N)
+        store_words(N - CH, N)
         for q in range(4):
             eng = nc.sync if q < 2 else nc.scalar
             eng.dma_start(out=scale_rows[4 * q:4 * q + 4, :], in_=y_scales[32 * q:32 * q + 4, :].bitcast(I32))

@@ -75,7 +75,8 @@ def tile_rows_pl_ggelu_kernel(tc, x, w, r, out_0, out_1, out_2):
             )
 
         load_w()
-        load_x(0, 2)
+        load_x(0, 1)
+        load_x(1, 1)
         load_x(2, 2)
 
         w_codes = sb.tile([P, M + 2 * R], U32, name="w_codes", align_bytes=64)
@@ -115,14 +116,14 @@ def tile_rows_pl_ggelu_kernel(tc, x, w, r, out_0, out_1, out_2):
         round_w()
         load_pair(0, 0, "raw_w")
         load_pair(1, 0, "raw_r0")
-        quantise_w(0)
         round_first(0)
         round_first(1)
-        quantise_w(1)
+        quantise_w(0)
         quantise_first(0)
         quantise_first(1)
+        quantise_w(1)
         round_x(1)
-        load_second_half("raw_x0")
+        load_second_half("raw_x1")
         quantise_x(1)
         round_x(2)
         round_x(3)
@@ -230,9 +231,8 @@ def tile_rows_pl_ggelu_kernel(tc, x, w, r, out_0, out_1, out_2):
         round_pair(6)
         round_pair(7)
         quantise_y(2)
-        store_words(HALF, N - CH)
         quantise_y(3)
-        store_words(N - CH, N)
+        store_words(HALF, N)
         for q in range(4):
             eng = nc.sync if q < 2 else nc.scalar
             eng.dma_start(out=scale_rows[4 * q:4 * q + 4, :], in_=y_scales[32 * q:32 * q + 4, :].bitcast(I32))

@@ -193,9 +193,9 @@ def tile_rows_pl_ggelu_kernel(tc, x, w, r, out_0, out_1, out_2):
         def round_chunk(c):
             interleave(y_bf[c][:], y[:, :, c * CH:(c + 1) * CH])
 
-        def round_pair(i):
+        def round_pair(i, copy):
             pair, c = pieces[i]
-            nc.vector.tensor_copy(
+            copy(
                 out=y_bf[c][:, :, 2 * pair:2 * pair + 2],
                 in_=y[:, 2 * pair:2 * pair + 2, c * CH:(c + 1) * CH].rearrange("p s n -> p n s"),
             )
@@ -210,29 +210,33 @@ def tile_rows_pl_ggelu_kernel(tc, x, w, r, out_0, out_1, out_2):
         def store_words(lo, hi):
             nc.sync.dma_start(out=word_rows[:, lo:hi], in_=y_codes[:, lo:hi].bitcast(I32))
 
+        def store_scales(q, eng):
+            eng.dma_start(out=scale_rows[4 * q:4 * q + 4, :], in_=y_scales[32 * q:32 * q + 4, :].bitcast(I32))
+
         add(0)
-        add(1)
-        round_chunk(0)
         add(2)
+        add(1)
         add(3)
         store_y(0, PACK, 0, HALF)
-        quantise_y(0)
+        round_chunk(0)
         round_chunk(1)
+        quantise_y(0)
         add(4)
         add(5)
         store_y(0, 2, HALF, N)
-        round_pair(4)
+        round_pair(5, nc.scalar.copy)
         quantise_y(1)
         store_words(0, HALF)
-        round_pair(5)
+        round_pair(4, nc.vector.tensor_copy)
         add(6)
         add(7)
         store_y(2, PACK, HALF, N)
-        round_pair(6)
-        round_pair(7)
+        round_pair(6, nc.vector.tensor_copy)
+        round_pair(7, nc.vector.tensor_copy)
         quantise_y(2)
         quantise_y(3)
+        store_scales(2, nc.scalar)
+        store_scales(3, nc.scalar)
         store_words(HALF, N)
-        for q in range(4):
-            eng = nc.sync if q < 2 else nc.scalar
-            eng.dma_start(out=scale_rows[4 * q:4 * q + 4, :], in_=y_scales[32 * q:32 * q + 4, :].bitcast(I32))
+        store_scales(0, nc.sync)
+        store_scales(1, nc.sync)

from contextlib import ExitStack

import concourse.mybir as mybir

G, D, M, N = 2, 256, 256, 512
FLOPS = 2 * G * D * M * N

F32 = mybir.dt.float32
BF16 = mybir.dt.bfloat16
U32 = mybir.dt.uint32
I32 = mybir.dt.int32
U8 = mybir.dt.uint8
FP8X4 = mybir.dt.float8_e4m3fn_x4
GELU = mybir.ActivationFunctionType.Gelu_apprx_tanh
ADD = mybir.AluOpType.add

P = 128
R = 64
PACK = 4
CH = 128
NCH = N // CH
HALF = N // 2
PAD = 16


def tile_rows_pl_ggelu_kernel(tc, x, w, r, out_0, out_1, out_2):
    nc = tc.nc
    x_rows = x.rearrange("g (p j) n -> (g p) j n", j=PACK)
    w_rows = w.rearrange("g (p j) m -> (g p) j m", j=PACK)
    r_rows = r.rearrange("g (p t) n -> (g p) t n", t=PACK)
    y_rows = out_0.rearrange("(p t) n -> p t n", t=PACK)
    word_rows = out_1.rearrange("s p n u -> p (s n u)").bitcast(I32)
    scale_rows = out_2.rearrange("s f n -> (s f) n").bitcast(I32)

    with ExitStack() as ctx:
        sb = ctx.enter_context(tc.tile_pool(name="sb", bufs=1))
        ps = ctx.enter_context(tc.psum_pool(name="ps", bufs=1))
        ctx.enter_context(tc.manual_schedule())

        x_raw = {}
        r_raw = {}
        w_raw = sb.tile([P, PACK, M], F32, name="w_raw", tag="raw_w", align_bytes=64)

        def load_w():
            nc.sync.dma_start(out=w_raw[:], in_=w_rows)

        def load_x(lo, n):
            xt = sb.tile([P, PACK, n * CH + PAD], F32, name="x_raw%d" % lo, tag="raw_x%d" % lo, align_bytes=64)
            nc.sync.dma_start(out=xt[:, :, 0:n * CH], in_=x_rows[:, :, lo * CH:(lo + n) * CH])
            for q in range(n):
                x_raw[lo + q] = xt[:, :, q * CH:(q + 1) * CH]

        def load_pair(pair, h, tag):
            rt = sb.tile([P, 2, HALF], F32, name="r_raw%d_%d" % (pair, h), tag=tag, align_bytes=64)
            nc.sync.dma_start(out=rt[:], in_=r_rows[:, 2 * pair:2 * pair + 2, h * HALF:(h + 1) * HALF])
            for c in range(2):
                r_raw[(pair, 2 * h + c)] = rt[:, :, c * CH:(c + 1) * CH]

        def load_second_half(tag):
            rt = sb.tile([P, PACK, HALF], F32, name="r_second", tag=tag, align_bytes=64)
            nc.sync.dma_start(out=rt[:], in_=r_rows[:, :, HALF:N])
            for pair in range(2):
                for c in range(2):
                    r_raw[(pair, 2 + c)] = rt[:, 2 * pair:2 * pair + 2, c * CH:(c + 1) * CH]

        def interleave(dst, src):
            nc.vector.tensor_copy(
                out=dst.rearrange("p (c i) j -> p c j i", i=PACK),
                in_=src.rearrange("p j (c i) -> p c j i", i=PACK),
            )

        def quantise(codes, scales, grouped):
            nc.vector.quantize_mx(
                out=codes.bitcast(FP8X4), scales=scales, in_=grouped.rearrange("p n j -> p (n j)")
            )

        load_w()
        load_x(0, 1)
        load_x(1, 1)
        load_x(2, 2)

        w_codes = sb.tile([P, M + 2 * R], U32, name="w_codes", align_bytes=64)
        w_scales = sb.tile([P, M + 2 * R], U8, name="w_scales", align_bytes=64)
        nc.vector.memset(w_codes[:], 0)
        nc.vector.memset(w_scales[:].bitcast(U32), 0)
        w_bf = sb.tile([P, PACK, R, PACK], BF16, name="w_bf", align_bytes=64)
        x_bf = {c: sb.tile([P, CH, PACK], BF16, name="x_bf%d" % c, align_bytes=64) for c in range(1, NCH)}
        x_codes = [sb.tile([P, CH], U32, name="x_codes%d" % c, align_bytes=64) for c in range(NCH)]
        x_scales = [sb.tile([P, CH], U8, name="x_scales%d" % c, align_bytes=64) for c in range(NCH)]

        def round_w():
            nc.vector.tensor_copy(
                out=w_bf[:].rearrange("p t m j -> p m t j"),
                in_=w_raw[:].rearrange("p j (m t) -> p m t j", t=PACK),
            )

        def quantise_w(pair):
            cols = slice(R + pair * P, R + (pair + 1) * P)
            slices = w_bf[:, 2 * pair:2 * pair + 2]
            quantise(w_codes[:, cols], w_scales[:, cols], slices.rearrange("p t m j -> p (t m) j"))

        def round_x(c):
            interleave(x_bf[c][:], x_raw[c])

        x_bf_first = [sb.tile([P, R, PACK], BF16, name="x_bf_first%d" % k, align_bytes=64) for k in range(2)]

        def round_first(k):
            interleave(x_bf_first[k][:], x_raw[0][:, :, k * R:(k + 1) * R])

        def quantise_first(k):
            quantise(x_codes[0][:, k * R:(k + 1) * R], x_scales[0][:, k * R:(k + 1) * R], x_bf_first[k][:])

        def quantise_x(c):
            quantise(x_codes[c][:], x_scales[c][:], x_bf[c][:])

        round_w()
        load_pair(0, 0, "raw_w")
        load_pair(1, 0, "raw_r0")
        round_first(0)
        round_first(1)
        quantise_w(0)
        quantise_first(0)
        quantise_first(1)
        quantise_w(1)
        round_x(1)
        load_second_half("raw_x1")
        quantise_x(1)
        round_x(2)
        round_x(3)
        quantise_x(2)
        quantise_x(3)

        pieces = [(0, 0), (1, 0), (0, 1), (1, 1), (0, 2), (0, 3), (1, 2), (1, 3)]
        z = {}
        opened = [0, 0]

        def passes(g, todo, slots=(0, 1)):
            bank = ps.tile(
                [P, len(todo), len(slots), CH], F32, name="z%d_%d" % (opened[g], g), tag="bank%d_%d" % (opened[g] % 4, g)
            )
            opened[g] = opened[g] + 1
            rows = slice(g * R, (g + 1) * R)
            for k, i in enumerate(todo):
                pair, c = pieces[i]
                z[(i, g, slots)] = bank[:, k, :, :]
                for n, s in enumerate(slots):
                    first = R * (2 * pair + s + 1 - g)
                    nc.tensor.matmul_mx(
                        out=bank[:, k, n, :],
                        lhsT=w_codes[rows, first:first + P].bitcast(FP8X4),
                        lhsT_scale=w_scales[rows, first:first + P],
                        rhs=x_codes[c][rows, :].bitcast(FP8X4),
                        rhs_scale=x_scales[c][rows, :],
                        start=True,
                        stop=True,
                    )

        act = [sb.tile([P, 2, CH], F32, name="act%d" % i) for i in range(len(pieces))]

        def gelu(i, g, slots=(0, 1)):
            rows = slice(0, (g + 1) * R)
            nc.scalar.activation(out=act[i][rows, slots[0]:slots[-1] + 1], in_=z[(i, g, slots)][rows], func=GELU)

        for s in range(2):
            passes(1, (0,), (s,))
            gelu(0, 1, (s,))
        for g, i in ((1, 1), (0, 0), (0, 1)):
            passes(g, (i,))
            gelu(i, g)
        for step in range(1, 4):
            todo = (2 * step, 2 * step + 1)
            for i in todo:
                for g in (0, 1):
                    passes(g, (i,))
            for g in (1, 0):
                for i in todo:
                    gelu(i, g)

        y = sb.tile([P, PACK, N + PAD], F32, name="y")
        y_bf = [sb.tile([P, CH, PACK], BF16, name="y_bf%d" % c, align_bytes=64) for c in range(NCH)]
        y_codes = sb.tile([P, N], U32, name="y_codes", align_bytes=64)
        y_scales = sb.tile([P, N], U8, name="y_scales", align_bytes=64)

        def add(i):
            pair, c = pieces[i]
            nc.vector.tensor_tensor(
                out=y[:, 2 * pair:2 * pair + 2, c * CH:(c + 1) * CH],
                in0=act[i][:],
                in1=r_raw[(pair, c)],
                op=ADD,
            )

        def round_chunk(c):
            interleave(y_bf[c][:], y[:, :, c * CH:(c + 1) * CH])

        def round_pair(i, copy):
            pair, c = pieces[i]
            copy(
                out=y_bf[c][:, :, 2 * pair:2 * pair + 2],
                in_=y[:, 2 * pair:2 * pair + 2, c * CH:(c + 1) * CH].rearrange("p s n -> p n s"),
            )

        def quantise_y(c):
            cols = slice(c * CH, (c + 1) * CH)
            quantise(y_codes[:, cols], y_scales[:, cols], y_bf[c][:])

        def store_y(first, last, lo, hi):
            nc.sync.dma_start(out=y_rows[:, first:last, lo:hi], in_=y[:, first:last, lo:hi])

        def store_words(lo, hi):
            nc.sync.dma_start(out=word_rows[:, lo:hi], in_=y_codes[:, lo:hi].bitcast(I32))

        def store_scales(q, eng):
            eng.dma_start(out=scale_rows[4 * q:4 * q + 4, :], in_=y_scales[32 * q:32 * q + 4, :].bitcast(I32))

        add(0)
        add(2)
        add(1)
        add(3)
        store_y(0, PACK, 0, HALF)
        round_chunk(0)
        round_chunk(1)
        quantise_y(0)
        add(4)
        add(5)
        store_y(0, 2, HALF, N)
        round_pair(5, nc.scalar.copy)
        quantise_y(1)
        store_words(0, HALF)
        round_pair(4, nc.vector.tensor_copy)
        add(6)
        add(7)
        store_y(2, PACK, HALF, N)
        round_pair(6, nc.vector.tensor_copy)
        round_pair(7, nc.vector.tensor_copy)
        quantise_y(2)
        quantise_y(3)
        store_scales(2, nc.scalar)
        store_scales(3, nc.scalar)
        store_words(HALF, N)
        store_scales(0, nc.sync)
        store_scales(1, nc.sync)
